import numpy as np
import ml_dtypes


def mxq(x, axis, fmt="e4m3"):
    dtype, down = {"e4m3": (ml_dtypes.float8_e4m3fn, 7), "e5m2": (ml_dtypes.float8_e5m2, 14)}[fmt]
    v = np.moveaxis(np.asarray(x, np.float32).astype(ml_dtypes.bfloat16).astype(np.float64), axis, -1)
    blocks = v.reshape(v.shape[:-1] + (-1, 32))
    amax = np.abs(blocks).max(-1, keepdims=True)
    byte = np.maximum(np.where(amax > 0, np.frexp(amax)[1] - 1 + 127, 0) - down, 1)
    scale = np.exp2(byte - 127.0)
    codes = (blocks / scale).astype(np.float32).astype(dtype).astype(np.float64)
    return np.moveaxis((codes * scale).reshape(v.shape), -1, axis)


WIDE = False


def mx_kscale(k):
    if not WIDE:
        return np.ones(k)
    levels = np.array([10, -10, 5, -5, 0])
    if k % 512:
        return np.exp2(np.random.permutation(np.resize(levels, k // 32))).repeat(32)
    a = np.empty((k // 512, 16))
    for p in range(k // 512):
        a[p, :8] = np.random.permutation(np.resize(levels, 8))
        for g in range(8):
            far = levels[np.abs(levels - a[p, g]) >= 10]
            a[p, g + 8] = far[np.random.randint(len(far))]
    return np.exp2(a.ravel()).repeat(32)


def f64(x):
    return np.asarray(x).astype(np.float64)


def striped(idx):
    return np.tile(idx.reshape(-1, 16).T, (8, 1)).astype(np.uint16)


def unstriped(offs):
    return offs[:16].T.reshape(-1).astype(np.int64)


def gelu(v):
    return 0.5 * v * (1.0 + np.tanh(np.sqrt(2.0 / np.pi) * (v + 0.044715 * v**3)))


K, T, E, C, H, N = 1024, 512, 4, 256, 1024, 128


def by_expert(wq, xq):
    return np.concatenate([wq[e].T @ xq[:, e * C:(e + 1) * C] for e in range(E)], axis=1)


def setup_inputs():
    n = np.random.standard_normal
    s = mx_kscale(K)[:, None]
    u = mx_kscale(H)
    first = np.random.permutation(np.repeat(np.arange(E), T // E))
    second = (first + 1 + np.random.permutation(np.repeat(np.arange(E - 1), -(-T // (E - 1)))[:T])) % E
    while np.bincount(second, minlength=E).max() != T // E:
        load = np.bincount(second, minlength=E); hi, lo = int(load.argmax()), int(load.argmin())
        t = np.flatnonzero((second == hi) & (first != lo))[0]; second[t] = lo
    slot_token = np.empty(E * C, np.int64); pos = np.empty((2, T), np.int64); fill = np.zeros(E, np.int64)
    place = np.stack([np.random.permutation(C) for _ in range(E)])
    for r, deal in enumerate((first, second)):
        for t in np.random.permutation(T):
            e = deal[t]; j = e * C + place[e, fill[e]]; fill[e] += 1; slot_token[j] = t; pos[r, t] = j
    g = np.random.uniform(0.2, 0.8, T)
    w_slot = np.empty(E * C); w_slot[pos[0]] = g; w_slot[pos[1]] = 1.0 - g
    return {
        "xT": (n((K, T)) * s).astype(np.float32),
        "w1": (n((E, K, H)) / np.sqrt(K) / s[None] * u[None, None, :]).astype(np.float32),
        "w2": (n((E, H, N)) / np.sqrt(H) / u[None, :, None]).astype(np.float32),
        "gate": np.tile(w_slot, (K, 1)).astype(np.float32),
        "offs": striped(slot_token),
        "pos1": striped(pos[0]),
        "pos2": striped(pos[1]),
    }


def reference(xT, w1, w2, gate, offs, pos1, pos2):
    idx = unstriped(offs)
    xq = mxq(f64(gate) * f64(xT)[:, idx], 0, "e4m3")
    h = gelu(by_expert(mxq(f64(w1), 1, "e4m3"), xq))
    y = by_expert(mxq(f64(w2), 1, "e4m3"), mxq(h, 0, "e4m3"))
    return y[:, unstriped(pos1)] + y[:, unstriped(pos2)]

@@ -1,0 +1,182 @@
+from contextlib import ExitStack
+
+import concourse.mybir as mybir
+
+K, T, E, C, H, N = 1024, 512, 4, 256, 1024, 128
+S = E * C
+FLOPS = 2 * S * (K * H + H * N)
+BYTES = 4 * (K * T + E * K * H + E * H * N + S + N * T) + 2 * 128 * (S + 2 * T) // 16
+
+F32 = mybir.dt.float32
+BF16 = mybir.dt.bfloat16
+U32 = mybir.dt.uint32
+U16 = mybir.dt.uint16
+U8 = mybir.dt.uint8
+FP8X4 = mybir.dt.float8_e4m3fn_x4
+MULT = mybir.AluOpType.mult
+ADD = mybir.AluOpType.add
+GELU = mybir.ActivationFunctionType.Gelu_apprx_tanh
+
+P = 128
+PACK = 4
+KP = P * PACK
+G = K // KP
+W1_ON_SCALAR = (0, 1, 2, 3, 5, 6, 7, 10, 12)
+X_ON_SCALAR = ((0, 0), (1, 0), (2, 0), (0, 1), (1, 1), (2, 1))
+AFTER = {0: 4, 2: 12}
+LOADS = "offs gate x00 x01 x02 x03 w00 x10 x11 x12 x13 w01 pos w10 w11 w20 w21 w30 w310 w311 v0 v1 v2 v3".split()
+TEXT = "T00 T10 T20 T30 W000 W001 T01 W010 W011 T11 T21 T31 W100 W101 H00 H01 W110 W111 W200 W201 H10 H11 W210 W211 W300 W301 H20 H21 W310 H30 W311 H31 V0 Y0 V1 Y1 V2 Y2 V3 Y3".split()
+W2_ON_SCALAR = (0, 1)
+
+
+def tile_moe_pre_mlp_gelu_kernel(tc, xT, w1, w2, gate, offs, pos1, pos2, out):
+    nc = tc.nc
+
+    def cast(on_scalar, dst, src):
+        if on_scalar:
+            nc.scalar.copy(dst, src)
+        else:
+            nc.vector.tensor_copy(dst, src)
+
+    with ExitStack() as ctx:
+        keep = ctx.enter_context(tc.tile_pool(name="keep", bufs=1))
+        ring = ctx.enter_context(tc.tile_pool(name="ring", bufs=2))
+        psum = ctx.enter_context(tc.psum_pool(name="psum", bufs=1))
+
+        def quantize(src, width, tag, bufs):
+            codes = ring.tile([P, width], U32, name=tag + "_codes", bufs=bufs, align_bytes=64)
+            scales = ring.tile([P, width], U8, name=tag + "_scales", bufs=bufs, align_bytes=64)
+            nc.vector.quantize_mx(out=codes[:].bitcast(FP8X4), scales=scales[:], in_=src)
+            return codes, scales
+
+        offs_sb = keep.tile([P, S // 16], U16, name="offs_sb")
+        pos1_sb = keep.tile([P, T // 16], U16, name="pos1_sb")
+        pos2_sb = keep.tile([P, T // 16], U16, name="pos2_sb")
+        gate_sb = keep.tile([P, S], F32, name="gate_sb")
+        x_rows = xT.rearrange("(g p j) t -> g j p t", g=G, j=PACK)
+        x_sb = {}
+        w1_raw = {}
+        w2_raw = {}
+
+        for item in LOADS:
+            n = [int(ch) for ch in item[1:]] if item[0] in "xwv" else []
+            if item == "offs":
+                nc.sync.dma_start(offs_sb[:], offs)
+            elif item == "gate":
+                nc.sync.dma_start(gate_sb[:], gate[0:P, :])
+            elif item == "pos":
+                nc.sync.dma_start(pos1_sb[:], pos1)
+                nc.sync.dma_start(pos2_sb[:], pos2)
+            elif item[0] == "x":
+                g, j = n
+                x_sb[g, j] = keep.tile([P, T], F32, name="x_%d_%d" % (g, j))
+                nc.sync.dma_start(x_sb[g, j][:], x_rows[g, j])
+            elif item[0] == "v":
+                e = n[0]
+                w2_raw[e] = keep.tile([P, G, PACK, N], F32, name="w2_raw_%d" % e)
+                nc.sync.dma_start(w2_raw[e][:], w2[e].rearrange("(g p j) n -> p g j n", g=G, j=PACK))
+            else:
+                e, g = n[0], n[1]
+                if (e, g) not in w1_raw:
+                    w1_raw[e, g] = ring.tile([P, PACK, H], F32, name="w1_raw", bufs=6, align_bytes=64)
+                rows = w1[e, g * KP : (g + 1) * KP, :].rearrange("(p j) c -> p j c", j=PACK)
+                cols = slice(0, H) if len(n) == 2 else slice(n[2] * KP, (n[2] + 1) * KP)
+                nc.sync.dma_start(w1_raw[e, g][:, :, cols], rows[:, :, cols])
+
+        xq = {}
+        w1q = {}
+        w2q = {}
+        hq = {}
+
+        def tokens(e, g):
+            picked = ring.tile([P, PACK, C], F32, name="picked", bufs=2)
+            for j in range(PACK):
+                nc.vector.tensor_tensor(
+                    picked[:, j, :],
+                    x_sb[g, j][:].indirect(offs_sb[:, e * C // 16 : (e + 1) * C // 16]),
+                    gate_sb[:, e * C : (e + 1) * C],
+                    MULT,
+                )
+            xb = ring.tile([P, C, PACK], BF16, name="xb", bufs=1, align_bytes=64)
+            cast(
+                (e, g) in X_ON_SCALAR,
+                xb[:].rearrange("p (c i) j -> p c j i", i=4),
+                picked[:].rearrange("p j (c i) -> p c j i", i=4),
+            )
+            xq[e, g] = quantize(xb[:].rearrange("p c j -> p (c j)"), C, "xq", E * G)
+
+        def weights1(e, g, u):
+            wb = ring.tile([P, PACK, P, PACK], BF16, name="wb", bufs=5, align_bytes=64)
+            cast(
+                (e * G + g) * G + u in W1_ON_SCALAR,
+                wb[:].rearrange("p t m j -> p m j t"),
+                w1_raw[e, g][:, :, u * KP : (u + 1) * KP].rearrange("p j (m t) -> p m j t", t=PACK),
+            )
+            w1q[e, g, u] = quantize(wb[:].rearrange("p t m j -> p (t m j)"), KP, "w1q", 4)
+
+        def hidden(e, u):
+            if e in AFTER:
+                k = AFTER[e]
+                c0 = (k % 2) * KP
+                flat = w1_raw[k // 4, (k // 2) % 2][:, u, c0 : c0 + KP].bitcast(BF16)
+            else:
+                own = ring.tile([P, C * PACK], BF16, name="hb", bufs=3, align_bytes=64)
+                flat = own[:]
+            hb = flat.rearrange("p (c t) -> p c t", t=PACK)
+            for s0 in range(0, C, P):
+                acc = psum.tile([P, PACK, P], F32, name="acc", bufs=6)
+                for t in range(PACK):
+                    for g in range(G):
+                        w_codes, w_scales = w1q[e, g, u]
+                        x_codes, x_scales = xq[e, g]
+                        nc.tensor.matmul_mx(
+                            out=acc[:, t, :],
+                            lhsT=w_codes[:, t * P : (t + 1) * P].bitcast(FP8X4),
+                            lhsT_scale=w_scales[:, t * P : (t + 1) * P],
+                            rhs=x_codes[:, s0 : s0 + P].bitcast(FP8X4),
+                            rhs_scale=x_scales[:, s0 : s0 + P],
+                            start=(g == 0),
+                            stop=(g == G - 1),
+                        )
+                nc.scalar.activation(hb[:, s0 : s0 + P, :], acc[:].rearrange("p t s -> p s t"), GELU)
+            hq[e, u] = quantize(flat, C, "hq", E * G)
+
+        def weights2(e):
+            wb = ring.tile([P, G, N, PACK], BF16, name="w2b", bufs=2, align_bytes=64)
+            cast(
+                e in W2_ON_SCALAR,
+                wb[:].rearrange("p g (c i) j -> p g c j i", i=4),
+                w2_raw[e][:].rearrange("p g j (c i) -> p g c j i", i=4),
+            )
+            w2q[e] = quantize(wb[:].rearrange("p g n j -> p (g n j)"), G * N, "w2q", E)
+
+        y_sb = keep.tile([P, S], F32, name="y_sb")
+
+        def results(e):
+            acc = psum.tile([P, C], F32, name="y_acc", bufs=2)
+            w_codes, w_scales = w2q[e]
+            for u in range(G):
+                h_codes, h_scales = hq[e, u]
+                nc.tensor.matmul_mx(
+                    out=acc[:],
+                    lhsT=w_codes[:, u * N : (u + 1) * N].bitcast(FP8X4),
+                    lhsT_scale=w_scales[:, u * N : (u + 1) * N],
+                    rhs=h_codes[:].bitcast(FP8X4),
+                    rhs_scale=h_scales[:],
+                    start=(u == 0),
+                    stop=(u == G - 1),
+                )
+            nc.scalar.copy(y_sb[:, e * C : (e + 1) * C], acc[:])
+
+        steps = {"T": tokens, "W": weights1, "H": hidden, "V": weights2, "Y": results}
+        for item in TEXT:
+            steps[item[0]](*[int(ch) for ch in item[1:]])
+
+        half = T // 2
+        for t0 in range(0, T, half):
+            first = ring.tile([P, half], F32, name="first", bufs=2)
+            both = ring.tile([P, half], F32, name="both", bufs=2)
+            cols = slice(t0 // 16, (t0 + half) // 16)
+            nc.vector.tensor_copy(first[:], y_sb[:].indirect(pos1_sb[:, cols]))
+            nc.vector.tensor_tensor(both[:], y_sb[:].indirect(pos2_sb[:, cols]), first[:], ADD)
+            nc.sync.dma_start(out[:, t0 : t0 + half], both[:])

@@ -21,12 +21,15 @@ P = 128
 PACK = 4
 KP = P * PACK
 G = K // KP
-W1_ON_SCALAR = (0, 1, 2, 3, 5, 6, 7, 10, 12)
-X_ON_SCALAR = ((0, 0), (1, 0), (2, 0), (0, 1), (1, 1), (2, 1))
-AFTER = {0: 4, 2: 12}
-LOADS = "offs gate x00 x01 x02 x03 w00 x10 x11 x12 x13 w01 pos w10 w11 w20 w21 w30 w310 w311 v0 v1 v2 v3".split()
-TEXT = "T00 T10 T20 T30 W000 W001 T01 W010 W011 T11 T21 T31 W100 W101 H00 H01 W110 W111 W200 W201 H10 H11 W210 W211 W300 W301 H20 H21 W310 H30 W311 H31 V0 Y0 V1 Y1 V2 Y2 V3 Y3".split()
-W2_ON_SCALAR = (0, 1)
+PAD = 16
+C2 = 2 * C
+W1_ON_SCALAR = (0, 1, 2, 3, 4, 5, 11, 13)
+W2_ON_SCALAR = (1,)
+X_ON_SCALAR = ((0, 0), (2, 0), (0, 1), (2, 1))
+X_AFTER = {(2, 0): 0, (0, 1): 0, (2, 1): 2}
+H_AFTER = {2: 6}
+LOADS = "offs ga x00 x01 x02 x03 gb w00 x10 x11 x12 x13 w01 pos w10 w11 w20 w21 w30 w310 w311 v0 v1 v2 v3".split()
+TEXT = "C00 C01 C20 C21 T00 W000 W001 T20 W010 W011 T01 W100 W101 T21 W110 W111 H00 H01 W200 W201 W210 W211 H10 H11 W300 W301 H20 H21 Z310 Z311 H30 H31 V0 V1 V2 V3 Y0 Y1 Y2 Y3".split()
 
 
 def tile_moe_pre_mlp_gelu_kernel(tc, xT, w1, w2, gate, offs, pos1, pos2, out):
@@ -62,63 +65,99 @@ def tile_moe_pre_mlp_gelu_kernel(tc, xT, w1, w2, gate, offs, pos1, pos2, out):
             n = [int(ch) for ch in item[1:]] if item[0] in "xwv" else []
             if item == "offs":
                 nc.sync.dma_start(offs_sb[:], offs)
-            elif item == "gate":
-                nc.sync.dma_start(gate_sb[:], gate[0:P, :])
+            elif item == "ga":
+                nc.sync.dma_start(gate_sb[:, 0:C2], gate[0:P, 0:C2])
+            elif item == "gb":
+                nc.sync.dma_start(gate_sb[:, C2:S], gate[0:P, C2:S])
             elif item == "pos":
                 nc.sync.dma_start(pos1_sb[:], pos1)
                 nc.sync.dma_start(pos2_sb[:], pos2)
             elif item[0] == "x":
                 g, j = n
-                x_sb[g, j] = keep.tile([P, T], F32, name="x_%d_%d" % (g, j))
-                nc.sync.dma_start(x_sb[g, j][:], x_rows[g, j])
+                x_sb[g, j] = keep.tile([P, T + PAD], F32, name="x_%d_%d" % (g, j))
+                nc.sync.dma_start(x_sb[g, j][:, 0:T], x_rows[g, j])
+                nc.vector.memset(x_sb[g, j][:, T : T + PAD], 0.0)
             elif item[0] == "v":
                 e = n[0]
-                w2_raw[e] = keep.tile([P, G, PACK, N], F32, name="w2_raw_%d" % e)
-                nc.sync.dma_start(w2_raw[e][:], w2[e].rearrange("(g p j) n -> p g j n", g=G, j=PACK))
+                if e == 0:
+                    w2_all = ring.tile([P, PACK * H], F32, name="w1_raw", bufs=6, align_bytes=64)
+                w2_raw[e] = w2_all[:, e * H : (e + 1) * H].rearrange("p (g j n) -> p g j n", g=G, j=PACK)
+                nc.sync.dma_start(w2_raw[e], w2[e].rearrange("(g p j) n -> p g j n", g=G, j=PACK))
             else:
                 e, g = n[0], n[1]
                 if (e, g) not in w1_raw:
-                    w1_raw[e, g] = ring.tile([P, PACK, H], F32, name="w1_raw", bufs=6, align_bytes=64)
+                    w1_raw[e, g] = ring.tile([P, PACK * H], F32, name="w1_raw", bufs=6, align_bytes=64)
                 rows = w1[e, g * KP : (g + 1) * KP, :].rearrange("(p j) c -> p j c", j=PACK)
                 cols = slice(0, H) if len(n) == 2 else slice(n[2] * KP, (n[2] + 1) * KP)
-                nc.sync.dma_start(w1_raw[e, g][:, :, cols], rows[:, :, cols])
+                nc.sync.dma_start(w1_raw[e, g][:].rearrange("p (j c) -> p j c", j=PACK)[:, :, cols], rows[:, :, cols])
 
         xq = {}
         w1q = {}
         w2q = {}
         hq = {}
+        picked = {}
 
-        def tokens(e, g):
-            picked = ring.tile([P, PACK, C], F32, name="picked", bufs=2)
+        def gather(e, g):
+            picked[e, g] = ring.tile([P, PACK * C2], F32, name="picked", bufs=3, align_bytes=64)
             for j in range(PACK):
                 nc.vector.tensor_tensor(
-                    picked[:, j, :],
-                    x_sb[g, j][:].indirect(offs_sb[:, e * C // 16 : (e + 1) * C // 16]),
-                    gate_sb[:, e * C : (e + 1) * C],
+                    picked[e, g][:, j * C2 : (j + 1) * C2],
+                    x_sb[g, j][:].indirect(offs_sb[:, e * C // 16 : (e + 2) * C // 16]),
+                    gate_sb[:, e * C : (e + 2) * C],
                     MULT,
                 )
-            xb = ring.tile([P, C, PACK], BF16, name="xb", bufs=1, align_bytes=64)
+
+        def tokens(e, g):
+            if (e, g) not in picked:
+                gather(e, g)
+            if (e, g) in X_AFTER:
+                k = X_AFTER[e, g]
+                xb = w1_raw[k // 2, k % 2][:, g * H : (g + 1) * H].bitcast(BF16)
+            else:
+                own = ring.tile([P, C2 * PACK], BF16, name="xb", bufs=1, align_bytes=64)
+                xb = own[:]
             cast(
                 (e, g) in X_ON_SCALAR,
-                xb[:].rearrange("p (c i) j -> p c j i", i=4),
-                picked[:].rearrange("p j (c i) -> p c j i", i=4),
+                xb.rearrange("p (c i j) -> p c j i", i=4, j=PACK),
+                picked[e, g][:].rearrange("p (j c i) -> p c j i", i=4, j=PACK),
             )
-            xq[e, g] = quantize(xb[:].rearrange("p c j -> p (c j)"), C, "xq", E * G)
+            codes, scales = quantize(xb, C2, "xq", 4)
+            for i in range(2):
+                xq[e + i, g] = (codes[:, i * C : (i + 1) * C], scales[:, i * C : (i + 1) * C])
 
-        def weights1(e, g, u):
-            wb = ring.tile([P, PACK, P, PACK], BF16, name="wb", bufs=5, align_bytes=64)
+        def weights1(e, g, tp):
+            wb = ring.tile([P, 2048], BF16, name="wb", bufs=4, align_bytes=64)
+            src = w1_raw[e, g][:].rearrange("p (j m t) -> p m j t", j=PACK, t=PACK)
             cast(
-                (e * G + g) * G + u in W1_ON_SCALAR,
-                wb[:].rearrange("p t m j -> p m j t"),
-                w1_raw[e, g][:, :, u * KP : (u + 1) * KP].rearrange("p j (m t) -> p m j t", t=PACK),
+                (e * G + g) * 2 + tp in W1_ON_SCALAR,
+                wb[:].rearrange("p (t m j) -> p m j t", t=2, j=PACK),
+                src[:, :, :, 2 * tp : 2 * tp + 2],
             )
-            w1q[e, g, u] = quantize(wb[:].rearrange("p t m j -> p (t m j)"), KP, "w1q", 4)
+            codes, scales = quantize(wb[:], KP, "w1q", 10)
+            for u in range(G):
+                for tt in range(2):
+                    cols = slice((tt * G + u) * P, (tt * G + u + 1) * P)
+                    w1q[e, g, u, 2 * tp + tt] = (codes[:, cols], scales[:, cols])
+
+        def weights1_split(e, g, u):
+            wb = ring.tile([P, 2048], BF16, name="wb", bufs=4, align_bytes=64)
+            src = w1_raw[e, g][:].rearrange("p (j m t) -> p m j t", j=PACK, t=PACK)
+            for tp in range(2):
+                cast(
+                    tp == 1,
+                    wb[:, tp * 1024 : (tp + 1) * 1024].rearrange("p (t m j) -> p m j t", t=2, j=PACK),
+                    src[:, u * P : (u + 1) * P, :, 2 * tp : 2 * tp + 2],
+                )
+            codes, scales = quantize(wb[:], KP, "w1q", 10)
+            for t in range(PACK):
+                w1q[e, g, u, t] = (codes[:, t * P : (t + 1) * P], scales[:, t * P : (t + 1) * P])
 
         def hidden(e, u):
-            if e in AFTER:
-                k = AFTER[e]
-                c0 = (k % 2) * KP
-                flat = w1_raw[k // 4, (k // 2) % 2][:, u, c0 : c0 + KP].bitcast(BF16)
+            if H_AFTER.get(e) == "p":
+                flat = picked[2, 1][:, u * KP : (u + 1) * KP].bitcast(BF16)
+            elif e in H_AFTER:
+                k = H_AFTER[e]
+                flat = w1_raw[k // 2, k % 2][:, (u + 2) * KP : (u + 3) * KP].bitcast(BF16)
             else:
                 own = ring.tile([P, C * PACK], BF16, name="hb", bufs=3, align_bytes=64)
                 flat = own[:]
@@ -127,12 +166,12 @@ def tile_moe_pre_mlp_gelu_kernel(tc, xT, w1, w2, gate, offs, pos1, pos2, out):
                 acc = psum.tile([P, PACK, P], F32, name="acc", bufs=6)
                 for t in range(PACK):
                     for g in range(G):
-                        w_codes, w_scales = w1q[e, g, u]
+                        w_codes, w_scales = w1q[e, g, u, t]
                         x_codes, x_scales = xq[e, g]
                         nc.tensor.matmul_mx(
                             out=acc[:, t, :],
-                            lhsT=w_codes[:, t * P : (t + 1) * P].bitcast(FP8X4),
-                            lhsT_scale=w_scales[:, t * P : (t + 1) * P],
+                            lhsT=w_codes.bitcast(FP8X4),
+                            lhsT_scale=w_scales,
                             rhs=x_codes[:, s0 : s0 + P].bitcast(FP8X4),
                             rhs_scale=x_scales[:, s0 : s0 + P],
                             start=(g == 0),
@@ -146,7 +185,7 @@ def tile_moe_pre_mlp_gelu_kernel(tc, xT, w1, w2, gate, offs, pos1, pos2, out):
             cast(
                 e in W2_ON_SCALAR,
                 wb[:].rearrange("p g (c i) j -> p g c j i", i=4),
-                w2_raw[e][:].rearrange("p g j (c i) -> p g c j i", i=4),
+                w2_raw[e].rearrange("p g j (c i) -> p g c j i", i=4),
             )
             w2q[e] = quantize(wb[:].rearrange("p g n j -> p (g n j)"), G * N, "w2q", E)
 
@@ -168,7 +207,7 @@ def tile_moe_pre_mlp_gelu_kernel(tc, xT, w1, w2, gate, offs, pos1, pos2, out):
                 )
             nc.scalar.copy(y_sb[:, e * C : (e + 1) * C], acc[:])
 
-        steps = {"T": tokens, "W": weights1, "H": hidden, "V": weights2, "Y": results}
+        steps = {"C": gather, "T": tokens, "W": weights1, "Z": weights1_split, "H": hidden, "V": weights2, "Y": results}
         for item in TEXT:
             steps[item[0]](*[int(ch) for ch in item[1:]])
 

@@ -23,13 +23,13 @@ KP = P * PACK
 G = K // KP
 PAD = 16
 C2 = 2 * C
-W1_ON_SCALAR = (0, 1, 2, 3, 4, 5, 11, 13)
-W2_ON_SCALAR = (1,)
-X_ON_SCALAR = ((0, 0), (2, 0), (0, 1), (2, 1))
-X_AFTER = {(2, 0): 0, (0, 1): 0, (2, 1): 2}
-H_AFTER = {2: 6}
+W1_SHARE = (3, 3, 4, 1, 1, 0, 2)
+W2_ON_SCALAR = (0,)
+X_ON_SCALAR = ((0, 0), (2, 0), (2, 1))
+X_AFTER = {(2, 0): 0, (2, 1): 2}
+H_AFTER = {1: 4, 2: 6}
 LOADS = "offs ga x00 x01 x02 x03 gb w00 x10 x11 x12 x13 w01 pos w10 w11 w20 w21 w30 w310 w311 v0 v1 v2 v3".split()
-TEXT = "C00 C01 C20 C21 T00 W000 W001 T20 W010 W011 T01 W100 W101 T21 W110 W111 H00 H01 W200 W201 W210 W211 H10 H11 W300 W301 H20 H21 Z310 Z311 H30 H31 V0 V1 V2 V3 Y0 Y1 Y2 Y3".split()
+TEXT = "C00 C01 C20 C21 T00 F00 T20 F01 T01 F10 T21 F11 F20 J0 F21 F30 J1 J2 Z310 Z311 H30 H31 V0 V1 V2 V3 Y0 Y1 Y2 Y3".split()
 
 
 def tile_moe_pre_mlp_gelu_kernel(tc, xT, w1, w2, gate, offs, pos1, pos2, out):
@@ -76,7 +76,7 @@ def tile_moe_pre_mlp_gelu_kernel(tc, xT, w1, w2, gate, offs, pos1, pos2, out):
                 g, j = n
                 x_sb[g, j] = keep.tile([P, T + PAD], F32, name="x_%d_%d" % (g, j))
                 nc.sync.dma_start(x_sb[g, j][:, 0:T], x_rows[g, j])
-                nc.vector.memset(x_sb[g, j][:, T : T + PAD], 0.0)
+                nc.gpsimd.memset(x_sb[g, j][:, T : T + PAD], 0.0)
             elif item[0] == "v":
                 e = n[0]
                 if e == 0:
@@ -114,7 +114,7 @@ def tile_moe_pre_mlp_gelu_kernel(tc, xT, w1, w2, gate, offs, pos1, pos2, out):
                 k = X_AFTER[e, g]
                 xb = w1_raw[k // 2, k % 2][:, g * H : (g + 1) * H].bitcast(BF16)
             else:
-                own = ring.tile([P, C2 * PACK], BF16, name="xb", bufs=1, align_bytes=64)
+                own = ring.tile([P, C2 * PACK], BF16, name="stage", bufs=4, align_bytes=64)
                 xb = own[:]
             cast(
                 (e, g) in X_ON_SCALAR,
@@ -125,22 +125,28 @@ def tile_moe_pre_mlp_gelu_kernel(tc, xT, w1, w2, gate, offs, pos1, pos2, out):
             for i in range(2):
                 xq[e + i, g] = (codes[:, i * C : (i + 1) * C], scales[:, i * C : (i + 1) * C])
 
-        def weights1(e, g, tp):
-            wb = ring.tile([P, 2048], BF16, name="wb", bufs=4, align_bytes=64)
-            src = w1_raw[e, g][:].rearrange("p (j m t) -> p m j t", j=PACK, t=PACK)
-            cast(
-                (e * G + g) * 2 + tp in W1_ON_SCALAR,
-                wb[:].rearrange("p (t m j) -> p m j t", t=2, j=PACK),
-                src[:, :, :, 2 * tp : 2 * tp + 2],
-            )
-            codes, scales = quantize(wb[:], KP, "w1q", 10)
+        def weights1(e, g):
+            wb = ring.tile([P, 4096], BF16, name="stage", bufs=4, align_bytes=64)
+            src = w1_raw[e, g][:].rearrange("p (j u m t) -> p u m j t", j=PACK, u=G, t=PACK)
+            dst = wb[:].rearrange("p (u t m j) -> p u m j t", u=G, t=PACK, j=PACK)
+            share = W1_SHARE[e * G + g]
+            if share in (0, 4):
+                cast(share == 4, dst, src)
+            elif share == 2:
+                cast(False, dst[:, 0], src[:, 0])
+                cast(True, dst[:, 1], src[:, 1])
+            else:
+                cast(share == 3, dst[:, 0], src[:, 0])
+                cast(False, dst[:, 1, :, :, 0:2], src[:, 1, :, :, 0:2])
+                cast(True, dst[:, 1, :, :, 2:4], src[:, 1, :, :, 2:4])
+            codes, scales = quantize(wb[:], H, "w1q", 4)
             for u in range(G):
-                for tt in range(2):
-                    cols = slice((tt * G + u) * P, (tt * G + u + 1) * P)
-                    w1q[e, g, u, 2 * tp + tt] = (codes[:, cols], scales[:, cols])
+                for t in range(PACK):
+                    cols = slice((u * PACK + t) * P, (u * PACK + t + 1) * P)
+                    w1q[e, g, u, t] = (codes[:, cols], scales[:, cols])
 
         def weights1_split(e, g, u):
-            wb = ring.tile([P, 2048], BF16, name="wb", bufs=4, align_bytes=64)
+            wb = ring.tile([P, 2048], BF16, name="stage", bufs=4, align_bytes=64)
             src = w1_raw[e, g][:].rearrange("p (j m t) -> p m j t", j=PACK, t=PACK)
             for tp in range(2):
                 cast(
@@ -148,24 +154,16 @@ def tile_moe_pre_mlp_gelu_kernel(tc, xT, w1, w2, gate, offs, pos1, pos2, out):
                     wb[:, tp * 1024 : (tp + 1) * 1024].rearrange("p (t m j) -> p m j t", t=2, j=PACK),
                     src[:, u * P : (u + 1) * P, :, 2 * tp : 2 * tp + 2],
                 )
-            codes, scales = quantize(wb[:], KP, "w1q", 10)
+            codes, scales = quantize(wb[:], KP, "w1q", 4)
             for t in range(PACK):
                 w1q[e, g, u, t] = (codes[:, t * P : (t + 1) * P], scales[:, t * P : (t + 1) * P])
 
-        def hidden(e, u):
-            if H_AFTER.get(e) == "p":
-                flat = picked[2, 1][:, u * KP : (u + 1) * KP].bitcast(BF16)
-            elif e in H_AFTER:
-                k = H_AFTER[e]
-                flat = w1_raw[k // 2, k % 2][:, (u + 2) * KP : (u + 3) * KP].bitcast(BF16)
-            else:
-                own = ring.tile([P, C * PACK], BF16, name="hb", bufs=3, align_bytes=64)
-                flat = own[:]
+        def first_layer(e, u, flat):
             hb = flat.rearrange("p (c t) -> p c t", t=PACK)
             for s0 in range(0, C, P):
                 acc = psum.tile([P, PACK, P], F32, name="acc", bufs=6)
                 for t in range(PACK):
-                    for g in range(G):
+                    for g in reversed(range(G)):
                         w_codes, w_scales = w1q[e, g, u, t]
                         x_codes, x_scales = xq[e, g]
                         nc.tensor.matmul_mx(
@@ -174,11 +172,31 @@ def tile_moe_pre_mlp_gelu_kernel(tc, xT, w1, w2, gate, offs, pos1, pos2, out):
                             lhsT_scale=w_scales,
                             rhs=x_codes[:, s0 : s0 + P].bitcast(FP8X4),
                             rhs_scale=x_scales[:, s0 : s0 + P],
-                            start=(g == 0),
-                            stop=(g == G - 1),
+                            start=(g == G - 1),
+                            stop=(g == 0),
                         )
                 nc.scalar.activation(hb[:, s0 : s0 + P, :], acc[:].rearrange("p t s -> p s t"), GELU)
-            hq[e, u] = quantize(flat, C, "hq", E * G)
+
+        def hidden(e, u):
+            own = ring.tile([P, C * PACK], BF16, name="hb_last", bufs=2, align_bytes=64)
+            first_layer(e, u, own[:])
+            codes, scales = quantize(own[:], C, "hq_last", 2)
+            hq[e, u] = (codes[:], scales[:])
+
+        def hidden_both(e):
+            if H_AFTER.get(e) == "p":
+                flat = picked[2, 1][:, 0:H].bitcast(BF16)
+            elif e in H_AFTER:
+                k = H_AFTER[e]
+                flat = w1_raw[k // 2, k % 2][:, 2 * H : 3 * H].bitcast(BF16)
+            else:
+                own = ring.tile([P, G * C * PACK], BF16, name="stage", bufs=4, align_bytes=64)
+                flat = own[:]
+            for u in range(G):
+                first_layer(e, u, flat[:, u * C * PACK : (u + 1) * C * PACK])
+            codes, scales = quantize(flat, G * C, "hq", E - 1)
+            for u in range(G):
+                hq[e, u] = (codes[:, u * C : (u + 1) * C], scales[:, u * C : (u + 1) * C])
 
         def weights2(e):
             wb = ring.tile([P, G, N, PACK], BF16, name="w2b", bufs=2, align_bytes=64)
@@ -189,25 +207,33 @@ def tile_moe_pre_mlp_gelu_kernel(tc, xT, w1, w2, gate, offs, pos1, pos2, out):
             )
             w2q[e] = quantize(wb[:].rearrange("p g n j -> p (g n j)"), G * N, "w2q", E)
 
+        def weights2_pair(e):
+            wb = ring.tile([P, 2 * G, N, PACK], BF16, name="w2b", bufs=2, align_bytes=64)
+            src = w2_all[:, e * H : (e + 2) * H].rearrange("p (g j c i) -> p g c j i", g=2 * G, j=PACK, i=4)
+            cast(e in W2_ON_SCALAR, wb[:].rearrange("p g (c i) j -> p g c j i", i=4), src)
+            codes, scales = quantize(wb[:].rearrange("p g n j -> p (g n j)"), 2 * G * N, "w2q", 2)
+            for i in range(2):
+                w2q[e + i] = (codes[:, i * G * N : (i + 1) * G * N], scales[:, i * G * N : (i + 1) * G * N])
+
         y_sb = keep.tile([P, S], F32, name="y_sb")
 
         def results(e):
             acc = psum.tile([P, C], F32, name="y_acc", bufs=2)
             w_codes, w_scales = w2q[e]
-            for u in range(G):
+            for u in reversed(range(G)):
                 h_codes, h_scales = hq[e, u]
                 nc.tensor.matmul_mx(
                     out=acc[:],
                     lhsT=w_codes[:, u * N : (u + 1) * N].bitcast(FP8X4),
                     lhsT_scale=w_scales[:, u * N : (u + 1) * N],
-                    rhs=h_codes[:].bitcast(FP8X4),
-                    rhs_scale=h_scales[:],
-                    start=(u == 0),
-                    stop=(u == G - 1),
+                    rhs=h_codes.bitcast(FP8X4),
+                    rhs_scale=h_scales,
+                    start=(u == G - 1),
+                    stop=(u == 0),
                 )
             nc.scalar.copy(y_sb[:, e * C : (e + 1) * C], acc[:])
 
-        steps = {"C": gather, "T": tokens, "W": weights1, "Z": weights1_split, "H": hidden, "V": weights2, "Y": results}
+        steps = {"C": gather, "T": tokens, "F": weights1, "J": hidden_both, "Z": weights1_split, "H": hidden, "V": weights2, "U": weights2_pair, "Y": results}
         for item in TEXT:
             steps[item[0]](*[int(ch) for ch in item[1:]])
 

@@ -21,227 +21,214 @@ P = 128
 PACK = 4
 KP = P * PACK
 G = K // KP
-PAD = 16
-C2 = 2 * C
-W1_SHARE = (3, 3, 4, 1, 1, 0, 2)
-W2_ON_SCALAR = (0,)
-X_ON_SCALAR = ((0, 0), (2, 0), (2, 1))
-X_AFTER = {(2, 0): 0, (2, 1): 2}
-H_AFTER = {1: 4, 2: 6}
-LOADS = "offs ga x00 x01 x02 x03 gb w00 x10 x11 x12 x13 w01 pos w10 w11 w20 w21 w30 w310 w311 v0 v1 v2 v3".split()
-TEXT = "C00 C01 C20 C21 T00 F00 T20 F01 T01 F10 T21 F11 F20 J0 F21 F30 J1 J2 Z310 Z311 H30 H31 V0 V1 V2 V3 Y0 Y1 Y2 Y3".split()
+PER_COLUMN = 16
+PAIR = 2 * C
+SPARE = 16
+RUN = 4
+
+CHUNKS = E * G
+SCALAR_ALONE = 3
+VECTOR_ALONE = CHUNKS - 2
+RAW_BUFS = 6
+STAGE_BUFS = 6
+W1_CODE_BUFS = 5
+ACC_BANKS = 6
 
 
 def tile_moe_pre_mlp_gelu_kernel(tc, xT, w1, w2, gate, offs, pos1, pos2, out):
     nc = tc.nc
-
-    def cast(on_scalar, dst, src):
-        if on_scalar:
-            nc.scalar.copy(dst, src)
-        else:
-            nc.vector.tensor_copy(dst, src)
 
     with ExitStack() as ctx:
         keep = ctx.enter_context(tc.tile_pool(name="keep", bufs=1))
         ring = ctx.enter_context(tc.tile_pool(name="ring", bufs=2))
         psum = ctx.enter_context(tc.psum_pool(name="psum", bufs=1))
 
-        def quantize(src, width, tag, bufs):
-            codes = ring.tile([P, width], U32, name=tag + "_codes", bufs=bufs, align_bytes=64)
-            scales = ring.tile([P, width], U8, name=tag + "_scales", bufs=bufs, align_bytes=64)
+        def quantize(src, words, tag, bufs):
+            codes = ring.tile([P, words], U32, name=tag + "_codes", bufs=bufs, align_bytes=64)
+            scales = ring.tile([P, words], U8, name=tag + "_scales", bufs=bufs, align_bytes=64)
             nc.vector.quantize_mx(out=codes[:].bitcast(FP8X4), scales=scales[:], in_=src)
             return codes, scales
 
-        offs_sb = keep.tile([P, S // 16], U16, name="offs_sb")
-        pos1_sb = keep.tile([P, T // 16], U16, name="pos1_sb")
-        pos2_sb = keep.tile([P, T // 16], U16, name="pos2_sb")
+        def columns(operand, first, count):
+            codes, scales = operand
+            return codes[:, first : first + count], scales[:, first : first + count]
+
+        def multiply(acc, stationary, moving, start, stop):
+            nc.tensor.matmul_mx(
+                out=acc,
+                lhsT=stationary[0].bitcast(FP8X4),
+                lhsT_scale=stationary[1],
+                rhs=moving[0].bitcast(FP8X4),
+                rhs_scale=moving[1],
+                start=start,
+                stop=stop,
+            )
+
+        offs_sb = keep.tile([P, S // PER_COLUMN], U16, name="offs_sb")
+        pos1_sb = keep.tile([P, T // PER_COLUMN], U16, name="pos1_sb")
+        pos2_sb = keep.tile([P, T // PER_COLUMN], U16, name="pos2_sb")
         gate_sb = keep.tile([P, S], F32, name="gate_sb")
         x_rows = xT.rearrange("(g p j) t -> g j p t", g=G, j=PACK)
         x_sb = {}
         w1_raw = {}
-        w2_raw = {}
 
-        for item in LOADS:
-            n = [int(ch) for ch in item[1:]] if item[0] in "xwv" else []
-            if item == "offs":
-                nc.sync.dma_start(offs_sb[:], offs)
-            elif item == "ga":
-                nc.sync.dma_start(gate_sb[:, 0:C2], gate[0:P, 0:C2])
-            elif item == "gb":
-                nc.sync.dma_start(gate_sb[:, C2:S], gate[0:P, C2:S])
-            elif item == "pos":
-                nc.sync.dma_start(pos1_sb[:], pos1)
-                nc.sync.dma_start(pos2_sb[:], pos2)
-            elif item[0] == "x":
-                g, j = n
-                x_sb[g, j] = keep.tile([P, T + PAD], F32, name="x_%d_%d" % (g, j))
+        def load_tokens(g):
+            for j in range(PACK):
+                x_sb[g, j] = keep.tile([P, T + SPARE], F32, name="x_%d_%d" % (g, j))
                 nc.sync.dma_start(x_sb[g, j][:, 0:T], x_rows[g, j])
-                nc.gpsimd.memset(x_sb[g, j][:, T : T + PAD], 0.0)
-            elif item[0] == "v":
-                e = n[0]
-                if e == 0:
-                    w2_all = ring.tile([P, PACK * H], F32, name="w1_raw", bufs=6, align_bytes=64)
-                w2_raw[e] = w2_all[:, e * H : (e + 1) * H].rearrange("p (g j n) -> p g j n", g=G, j=PACK)
-                nc.sync.dma_start(w2_raw[e], w2[e].rearrange("(g p j) n -> p g j n", g=G, j=PACK))
-            else:
-                e, g = n[0], n[1]
-                if (e, g) not in w1_raw:
-                    w1_raw[e, g] = ring.tile([P, PACK * H], F32, name="w1_raw", bufs=6, align_bytes=64)
-                rows = w1[e, g * KP : (g + 1) * KP, :].rearrange("(p j) c -> p j c", j=PACK)
-                cols = slice(0, H) if len(n) == 2 else slice(n[2] * KP, (n[2] + 1) * KP)
-                nc.sync.dma_start(w1_raw[e, g][:].rearrange("p (j c) -> p j c", j=PACK)[:, :, cols], rows[:, :, cols])
+                nc.gpsimd.memset(x_sb[g, j][:, T : T + SPARE], 0.0)
 
+        def load_chunk(e, g, pieces):
+            w1_raw[e, g] = ring.tile([P, PACK * H], F32, name="raw", bufs=RAW_BUFS, align_bytes=64)
+            rows = w1[e, g * KP : (g + 1) * KP, :].rearrange("(p j) c -> p j c", j=PACK)
+            dst = w1_raw[e, g][:].rearrange("p (j c) -> p j c", j=PACK)
+            for c0 in range(0, H, H // pieces):
+                cols = slice(c0, c0 + H // pieces)
+                nc.sync.dma_start(dst[:, :, cols], rows[:, :, cols])
+
+        nc.sync.dma_start(offs_sb[:], offs)
+        nc.sync.dma_start(gate_sb[:, 0:PAIR], gate[0:P, 0:PAIR])
+        load_tokens(0)
+        nc.sync.dma_start(gate_sb[:, PAIR:S], gate[0:P, PAIR:S])
+        load_chunk(0, 0, 1)
+        load_tokens(1)
+        load_chunk(0, 1, 1)
+        nc.sync.dma_start(pos1_sb[:], pos1)
+        nc.sync.dma_start(pos2_sb[:], pos2)
+        for chunk in range(G, CHUNKS):
+            load_chunk(chunk // G, chunk % G, G if chunk == CHUNKS - 1 else 1)
+        w2_raw = ring.tile([P, E * G * PACK * N], F32, name="raw", bufs=RAW_BUFS, align_bytes=64)
+        w2_view = w2_raw[:].rearrange("p (e u j n) -> p e u j n", e=E, u=G, j=PACK)
+        for e in range(E):
+            nc.sync.dma_start(w2_view[:, e], w2[e].rearrange("(u p j) n -> p u j n", u=G, j=PACK))
+
+        picked = {}
         xq = {}
         w1q = {}
-        w2q = {}
         hq = {}
-        picked = {}
-
-        def gather(e, g):
-            picked[e, g] = ring.tile([P, PACK * C2], F32, name="picked", bufs=3, align_bytes=64)
-            for j in range(PACK):
-                nc.vector.tensor_tensor(
-                    picked[e, g][:, j * C2 : (j + 1) * C2],
-                    x_sb[g, j][:].indirect(offs_sb[:, e * C // 16 : (e + 2) * C // 16]),
-                    gate_sb[:, e * C : (e + 2) * C],
-                    MULT,
-                )
-
-        def tokens(e, g):
-            if (e, g) not in picked:
-                gather(e, g)
-            if (e, g) in X_AFTER:
-                k = X_AFTER[e, g]
-                xb = w1_raw[k // 2, k % 2][:, g * H : (g + 1) * H].bitcast(BF16)
-            else:
-                own = ring.tile([P, C2 * PACK], BF16, name="stage", bufs=4, align_bytes=64)
-                xb = own[:]
-            cast(
-                (e, g) in X_ON_SCALAR,
-                xb.rearrange("p (c i j) -> p c j i", i=4, j=PACK),
-                picked[e, g][:].rearrange("p (j c i) -> p c j i", i=4, j=PACK),
-            )
-            codes, scales = quantize(xb, C2, "xq", 4)
-            for i in range(2):
-                xq[e + i, g] = (codes[:, i * C : (i + 1) * C], scales[:, i * C : (i + 1) * C])
-
-        def weights1(e, g):
-            wb = ring.tile([P, 4096], BF16, name="stage", bufs=4, align_bytes=64)
-            src = w1_raw[e, g][:].rearrange("p (j u m t) -> p u m j t", j=PACK, u=G, t=PACK)
-            dst = wb[:].rearrange("p (u t m j) -> p u m j t", u=G, t=PACK, j=PACK)
-            share = W1_SHARE[e * G + g]
-            if share in (0, 4):
-                cast(share == 4, dst, src)
-            elif share == 2:
-                cast(False, dst[:, 0], src[:, 0])
-                cast(True, dst[:, 1], src[:, 1])
-            else:
-                cast(share == 3, dst[:, 0], src[:, 0])
-                cast(False, dst[:, 1, :, :, 0:2], src[:, 1, :, :, 0:2])
-                cast(True, dst[:, 1, :, :, 2:4], src[:, 1, :, :, 2:4])
-            codes, scales = quantize(wb[:], H, "w1q", 4)
-            for u in range(G):
-                for t in range(PACK):
-                    cols = slice((u * PACK + t) * P, (u * PACK + t + 1) * P)
-                    w1q[e, g, u, t] = (codes[:, cols], scales[:, cols])
-
-        def weights1_split(e, g, u):
-            wb = ring.tile([P, 2048], BF16, name="stage", bufs=4, align_bytes=64)
-            src = w1_raw[e, g][:].rearrange("p (j m t) -> p m j t", j=PACK, t=PACK)
-            for tp in range(2):
-                cast(
-                    tp == 1,
-                    wb[:, tp * 1024 : (tp + 1) * 1024].rearrange("p (t m j) -> p m j t", t=2, j=PACK),
-                    src[:, u * P : (u + 1) * P, :, 2 * tp : 2 * tp + 2],
-                )
-            codes, scales = quantize(wb[:], KP, "w1q", 4)
-            for t in range(PACK):
-                w1q[e, g, u, t] = (codes[:, t * P : (t + 1) * P], scales[:, t * P : (t + 1) * P])
-
-        def first_layer(e, u, flat):
-            hb = flat.rearrange("p (c t) -> p c t", t=PACK)
-            for s0 in range(0, C, P):
-                acc = psum.tile([P, PACK, P], F32, name="acc", bufs=6)
-                for t in range(PACK):
-                    for g in reversed(range(G)):
-                        w_codes, w_scales = w1q[e, g, u, t]
-                        x_codes, x_scales = xq[e, g]
-                        nc.tensor.matmul_mx(
-                            out=acc[:, t, :],
-                            lhsT=w_codes.bitcast(FP8X4),
-                            lhsT_scale=w_scales,
-                            rhs=x_codes[:, s0 : s0 + P].bitcast(FP8X4),
-                            rhs_scale=x_scales[:, s0 : s0 + P],
-                            start=(g == G - 1),
-                            stop=(g == 0),
-                        )
-                nc.scalar.activation(hb[:, s0 : s0 + P, :], acc[:].rearrange("p t s -> p s t"), GELU)
-
-        def hidden(e, u):
-            own = ring.tile([P, C * PACK], BF16, name="hb_last", bufs=2, align_bytes=64)
-            first_layer(e, u, own[:])
-            codes, scales = quantize(own[:], C, "hq_last", 2)
-            hq[e, u] = (codes[:], scales[:])
-
-        def hidden_both(e):
-            if H_AFTER.get(e) == "p":
-                flat = picked[2, 1][:, 0:H].bitcast(BF16)
-            elif e in H_AFTER:
-                k = H_AFTER[e]
-                flat = w1_raw[k // 2, k % 2][:, 2 * H : 3 * H].bitcast(BF16)
-            else:
-                own = ring.tile([P, G * C * PACK], BF16, name="stage", bufs=4, align_bytes=64)
-                flat = own[:]
-            for u in range(G):
-                first_layer(e, u, flat[:, u * C * PACK : (u + 1) * C * PACK])
-            codes, scales = quantize(flat, G * C, "hq", E - 1)
-            for u in range(G):
-                hq[e, u] = (codes[:, u * C : (u + 1) * C], scales[:, u * C : (u + 1) * C])
-
-        def weights2(e):
-            wb = ring.tile([P, G, N, PACK], BF16, name="w2b", bufs=2, align_bytes=64)
-            cast(
-                e in W2_ON_SCALAR,
-                wb[:].rearrange("p g (c i) j -> p g c j i", i=4),
-                w2_raw[e].rearrange("p g j (c i) -> p g c j i", i=4),
-            )
-            w2q[e] = quantize(wb[:].rearrange("p g n j -> p (g n j)"), G * N, "w2q", E)
-
-        def weights2_pair(e):
-            wb = ring.tile([P, 2 * G, N, PACK], BF16, name="w2b", bufs=2, align_bytes=64)
-            src = w2_all[:, e * H : (e + 2) * H].rearrange("p (g j c i) -> p g c j i", g=2 * G, j=PACK, i=4)
-            cast(e in W2_ON_SCALAR, wb[:].rearrange("p g (c i) j -> p g c j i", i=4), src)
-            codes, scales = quantize(wb[:].rearrange("p g n j -> p (g n j)"), 2 * G * N, "w2q", 2)
-            for i in range(2):
-                w2q[e + i] = (codes[:, i * G * N : (i + 1) * G * N], scales[:, i * G * N : (i + 1) * G * N])
-
         y_sb = keep.tile([P, S], F32, name="y_sb")
 
-        def results(e):
-            acc = psum.tile([P, C], F32, name="y_acc", bufs=2)
-            w_codes, w_scales = w2q[e]
-            for u in reversed(range(G)):
-                h_codes, h_scales = hq[e, u]
-                nc.tensor.matmul_mx(
-                    out=acc[:],
-                    lhsT=w_codes[:, u * N : (u + 1) * N].bitcast(FP8X4),
-                    lhsT_scale=w_scales[:, u * N : (u + 1) * N],
-                    rhs=h_codes.bitcast(FP8X4),
-                    rhs_scale=h_scales,
-                    start=(u == G - 1),
-                    stop=(u == 0),
+        def gather_width(pair, g):
+            return C if (pair, g) == (0, 0) else PAIR
+
+        def gather(pair, g):
+            picked[pair, g] = ring.tile([P, PACK * PAIR], F32, name="stage", bufs=STAGE_BUFS, align_bytes=64)
+            width = gather_width(pair, g)
+            for s0 in range(0, PAIR, width):
+                slot = pair * PAIR + s0
+                for j in range(PACK):
+                    nc.vector.tensor_tensor(
+                        picked[pair, g][:, PACK * s0 + j * width : PACK * s0 + (j + 1) * width],
+                        x_sb[g, j][:].indirect(offs_sb[:, slot // PER_COLUMN : (slot + width) // PER_COLUMN]),
+                        gate_sb[:, slot : slot + width],
+                        MULT,
+                    )
+
+        def tokens(pair, g):
+            if pair == 0:
+                own = ring.tile([P, PAIR * PACK], BF16, name="xb", bufs=1, align_bytes=64)
+                xb = own[:]
+            else:
+                xb = w1_raw[g, 0][:, g * H : (g + 1) * H].bitcast(BF16)
+            copy = nc.vector.tensor_copy if (pair, g) == (0, G - 1) else nc.scalar.copy
+            width = gather_width(pair, g)
+            for s0 in range(0, PAIR, width):
+                cols = slice(PACK * s0, PACK * (s0 + width))
+                copy(
+                    xb[:, cols].rearrange("p (c r j) -> p c j r", r=RUN, j=PACK),
+                    picked[pair, g][:, cols].rearrange("p (j c r) -> p c j r", r=RUN, j=PACK),
                 )
+            quantised = quantize(xb, PAIR, "xq", 2 * G)
+            for i in range(2):
+                xq[2 * pair + i, g] = columns(quantised, i * C, C)
+
+        def weights1(e, g):
+            wb = ring.tile([P, PACK * H], BF16, name="stage", bufs=STAGE_BUFS, align_bytes=64)
+            src = w1_raw[e, g][:].rearrange("p (j u m t) -> p u m j t", j=PACK, u=G, t=PACK)
+            dst = wb[:].rearrange("p (u t m j) -> p u m j t", u=G, t=PACK, j=PACK)
+            chunk = e * G + g
+            if chunk < SCALAR_ALONE:
+                nc.scalar.copy(dst, src)
+            elif chunk == VECTOR_ALONE:
+                nc.vector.tensor_copy(dst, src)
+            else:
+                nc.vector.tensor_copy(dst[:, 0], src[:, 0])
+                nc.scalar.copy(dst[:, 1], src[:, 1])
+            quantised = quantize(wb[:], H, "w1q", W1_CODE_BUFS)
+            for u in range(G):
+                for t in range(PACK):
+                    w1q[e, g, u, t] = columns(quantised, (u * PACK + t) * P, P)
+
+        def weights1_half(e, g, u):
+            wb = ring.tile([P, PACK * KP], BF16, name="stage", bufs=STAGE_BUFS, align_bytes=64)
+            src = w1_raw[e, g][:].rearrange("p (j u m t) -> p u m j t", j=PACK, u=G, t=PACK)
+            dst = wb[:].rearrange("p (t m j) -> p m j t", t=PACK, j=PACK)
+            nc.vector.tensor_copy(dst[:, :, :, 0:2], src[:, u, :, :, 0:2])
+            nc.scalar.copy(dst[:, :, :, 2:4], src[:, u, :, :, 2:4])
+            quantised = quantize(wb[:], KP, "w1q", W1_CODE_BUFS)
+            for t in range(PACK):
+                w1q[e, g, u, t] = columns(quantised, t * P, P)
+
+        def first_layer(e, u, hb):
+            hb_view = hb.rearrange("p (c t) -> p c t", t=PACK)
+            for s0 in range(0, C, P):
+                acc = psum.tile([P, PACK, P], F32, name="acc", bufs=ACC_BANKS)
+                for t in range(PACK):
+                    for g in reversed(range(G)):
+                        multiply(acc[:, t, :], w1q[e, g, u, t], columns(xq[e, g], s0, P), g == G - 1, g == 0)
+                nc.scalar.activation(hb_view[:, s0 : s0 + P, :], acc[:].rearrange("p t s -> p s t"), GELU)
+
+        def hidden(e, spent):
+            hb = spent.bitcast(BF16)
+            for u in range(G):
+                first_layer(e, u, hb[:, u * C * PACK : (u + 1) * C * PACK])
+            quantised = quantize(hb, G * C, "hq", E - 1)
+            for u in range(G):
+                hq[e, u] = columns(quantised, u * C, C)
+
+        def hidden_half(e, u):
+            hb = ring.tile([P, C * PACK], BF16, name="hb_half", bufs=G, align_bytes=64)
+            first_layer(e, u, hb[:])
+            hq[e, u] = columns(quantize(hb[:], C, "hq_half", G), 0, C)
+
+        def second_layer(e):
+            wb = ring.tile([P, G, N, PACK], BF16, name="w2b", bufs=2, align_bytes=64)
+            copy = nc.scalar.copy if e == 0 else nc.vector.tensor_copy
+            copy(
+                wb[:].rearrange("p u (c r) j -> p u c j r", r=RUN),
+                w2_view[:, e].rearrange("p u j (c r) -> p u c j r", r=RUN),
+            )
+            w2q = quantize(wb[:].rearrange("p u n j -> p (u n j)"), G * N, "w2q", E)
+            acc = psum.tile([P, C], F32, name="y_acc", bufs=2)
+            for u in reversed(range(G)):
+                multiply(acc[:], columns(w2q, u * N, N), hq[e, u], u == G - 1, u == 0)
             nc.scalar.copy(y_sb[:, e * C : (e + 1) * C], acc[:])
 
-        steps = {"C": gather, "T": tokens, "F": weights1, "J": hidden_both, "Z": weights1_split, "H": hidden, "V": weights2, "U": weights2_pair, "Y": results}
-        for item in TEXT:
-            steps[item[0]](*[int(ch) for ch in item[1:]])
+        for g in range(G):
+            for pair in range(E // 2):
+                gather(pair, g)
+        for pair in range(E // 2):
+            for g in range(G):
+                tokens(pair, g)
+                weights1(pair, g)
+        free_part = slice(2 * H, 3 * H)
+        weights1(2, 0)
+        hidden(0, picked[1, G - 1][:, 0:H])
+        weights1(2, 1)
+        weights1(3, 0)
+        hidden(1, w1_raw[2, 1][:, free_part])
+        hidden(2, w1_raw[3, 0][:, free_part])
+        for u in range(G):
+            weights1_half(E - 1, G - 1, u)
+            hidden_half(E - 1, u)
+        for e in range(E):
+            second_layer(e)
 
         half = T // 2
         for t0 in range(0, T, half):
             first = ring.tile([P, half], F32, name="first", bufs=2)
             both = ring.tile([P, half], F32, name="both", bufs=2)
-            cols = slice(t0 // 16, (t0 + half) // 16)
-            nc.vector.tensor_copy(first[:], y_sb[:].indirect(pos1_sb[:, cols]))
-            nc.vector.tensor_tensor(both[:], y_sb[:].indirect(pos2_sb[:, cols]), first[:], ADD)
+            entries = slice(t0 // PER_COLUMN, (t0 + half) // PER_COLUMN)
+            nc.vector.tensor_copy(first[:], y_sb[:].indirect(pos1_sb[:, entries]))
+            nc.vector.tensor_tensor(both[:], y_sb[:].indirect(pos2_sb[:, entries]), first[:], ADD)
             nc.sync.dma_start(out[:, t0 : t0 + half], both[:])

@@ -144,20 +144,24 @@ def tile_moe_pre_mlp_gelu_kernel(tc, xT, w1, w2, gate, offs, pos1, pos2, out):
 
         def weights1(e, g):
             wb = ring.tile([P, PACK * H], BF16, name="stage", bufs=STAGE_BUFS, align_bytes=64)
-            src = w1_raw[e, g][:].rearrange("p (j u m t) -> p u m j t", j=PACK, u=G, t=PACK)
-            dst = wb[:].rearrange("p (u t m j) -> p u m j t", u=G, t=PACK, j=PACK)
             chunk = e * G + g
-            if chunk < SCALAR_ALONE:
-                nc.scalar.copy(dst, src)
-            elif chunk == VECTOR_ALONE:
-                nc.vector.tensor_copy(dst, src)
+            if chunk == VECTOR_ALONE:
+                nc.vector.tensor_copy(
+                    wb[:].rearrange("p (t m j) -> p m j t", t=PACK, j=PACK),
+                    w1_raw[e, g][:].rearrange("p (j m t) -> p m j t", j=PACK, t=PACK),
+                )
             else:
-                nc.vector.tensor_copy(dst[:, 0], src[:, 0])
-                nc.scalar.copy(dst[:, 1], src[:, 1])
+                src = w1_raw[e, g][:].rearrange("p (j m a b) -> p a m j b", j=PACK, a=2, b=2)
+                dst = wb[:].rearrange("p (a b m j) -> p a m j b", a=2, b=2, j=PACK)
+                if chunk < SCALAR_ALONE:
+                    nc.scalar.copy(dst, src)
+                else:
+                    nc.vector.tensor_copy(dst[:, 0], src[:, 0])
+                    nc.scalar.copy(dst[:, 1], src[:, 1])
             quantised = quantize(wb[:], H, "w1q", W1_CODE_BUFS)
             for u in range(G):
                 for t in range(PACK):
-                    w1q[e, g, u, t] = columns(quantised, (u * PACK + t) * P, P)
+                    w1q[e, g, u, t] = columns(quantised, (t * G + u) * P, P)
 
         def weights1_half(e, g, u):
             wb = ring.tile([P, PACK * KP], BF16, name="stage", bufs=STAGE_BUFS, align_bytes=64)

from contextlib import ExitStack

import concourse.mybir as mybir

K, T, E, C, H, N = 1024, 512, 4, 256, 1024, 128
S = E * C
FLOPS = 2 * S * (K * H + H * N)
BYTES = 4 * (K * T + E * K * H + E * H * N + S + N * T) + 2 * 128 * (S + 2 * T) // 16

F32 = mybir.dt.float32
BF16 = mybir.dt.bfloat16
U32 = mybir.dt.uint32
U16 = mybir.dt.uint16
U8 = mybir.dt.uint8
FP8X4 = mybir.dt.float8_e4m3fn_x4
MULT = mybir.AluOpType.mult
ADD = mybir.AluOpType.add
GELU = mybir.ActivationFunctionType.Gelu_apprx_tanh

P = 128
PACK = 4
KP = P * PACK
G = K // KP
PER_COLUMN = 16
PAIR = 2 * C
SPARE = 16
RUN = 4

CHUNKS = E * G
SCALAR_ALONE = 3
VECTOR_ALONE = CHUNKS - 2
RAW_BUFS = 6
STAGE_BUFS = 6
W1_CODE_BUFS = 5
ACC_BANKS = 6


def tile_moe_pre_mlp_gelu_kernel(tc, xT, w1, w2, gate, offs, pos1, pos2, out):
    nc = tc.nc

    with ExitStack() as ctx:
        keep = ctx.enter_context(tc.tile_pool(name="keep", bufs=1))
        ring = ctx.enter_context(tc.tile_pool(name="ring", bufs=2))
        psum = ctx.enter_context(tc.psum_pool(name="psum", bufs=1))

        def quantize(src, words, tag, bufs):
            codes = ring.tile([P, words], U32, name=tag + "_codes", bufs=bufs, align_bytes=64)
            scales = ring.tile([P, words], U8, name=tag + "_scales", bufs=bufs, align_bytes=64)
            nc.vector.quantize_mx(out=codes[:].bitcast(FP8X4), scales=scales[:], in_=src)
            return codes, scales

        def columns(operand, first, count):
            codes, scales = operand
            return codes[:, first : first + count], scales[:, first : first + count]

        def multiply(acc, stationary, moving, start, stop):
            nc.tensor.matmul_mx(
                out=acc,
                lhsT=stationary[0].bitcast(FP8X4),
                lhsT_scale=stationary[1],
                rhs=moving[0].bitcast(FP8X4),
                rhs_scale=moving[1],
                start=start,
                stop=stop,
            )

        offs_sb = keep.tile([P, S // PER_COLUMN], U16, name="offs_sb")
        pos1_sb = keep.tile([P, T // PER_COLUMN], U16, name="pos1_sb")
        pos2_sb = keep.tile([P, T // PER_COLUMN], U16, name="pos2_sb")
        gate_sb = keep.tile([P, S], F32, name="gate_sb")
        x_rows = xT.rearrange("(g p j) t -> g j p t", g=G, j=PACK)
        x_sb = {}
        w1_raw = {}

        def load_tokens(g):
            for j in range(PACK):
                x_sb[g, j] = keep.tile([P, T + SPARE], F32, name="x_%d_%d" % (g, j))
                nc.sync.dma_start(x_sb[g, j][:, 0:T], x_rows[g, j])
                nc.gpsimd.memset(x_sb[g, j][:, T : T + SPARE], 0.0)

        def load_chunk(e, g, pieces):
            w1_raw[e, g] = ring.tile([P, PACK * H], F32, name="raw", bufs=RAW_BUFS, align_bytes=64)
            rows = w1[e, g * KP : (g + 1) * KP, :].rearrange("(p j) c -> p j c", j=PACK)
            dst = w1_raw[e, g][:].rearrange("p (j c) -> p j c", j=PACK)
            for c0 in range(0, H, H // pieces):
                cols = slice(c0, c0 + H // pieces)
                nc.sync.dma_start(dst[:, :, cols], rows[:, :, cols])

        nc.sync.dma_start(offs_sb[:], offs)
        nc.sync.dma_start(gate_sb[:, 0:PAIR], gate[0:P, 0:PAIR])
        load_tokens(0)
        nc.sync.dma_start(gate_sb[:, PAIR:S], gate[0:P, PAIR:S])
        load_chunk(0, 0, 1)
        load_tokens(1)
        load_chunk(0, 1, 1)
        nc.sync.dma_start(pos1_sb[:], pos1)
        nc.sync.dma_start(pos2_sb[:], pos2)
        for chunk in range(G, CHUNKS):
            load_chunk(chunk // G, chunk % G, G if chunk == CHUNKS - 1 else 1)
        w2_raw = ring.tile([P, E * G * PACK * N], F32, name="raw", bufs=RAW_BUFS, align_bytes=64)
        w2_view = w2_raw[:].rearrange("p (e u j n) -> p e u j n", e=E, u=G, j=PACK)
        for e in range(E):
            nc.sync.dma_start(w2_view[:, e], w2[e].rearrange("(u p j) n -> p u j n", u=G, j=PACK))

        picked = {}
        xq = {}
        w1q = {}
        hq = {}
        y_sb = keep.tile([P, S], F32, name="y_sb")

        def gather_width(pair, g):
            return C if (pair, g) == (0, 0) else PAIR

        def gather(pair, g):
            picked[pair, g] = ring.tile([P, PACK * PAIR], F32, name="stage", bufs=STAGE_BUFS, align_bytes=64)
            width = gather_width(pair, g)
            for s0 in range(0, PAIR, width):
                slot = pair * PAIR + s0
                for j in range(PACK):
                    nc.vector.tensor_tensor(
                        picked[pair, g][:, PACK * s0 + j * width : PACK * s0 + (j + 1) * width],
                        x_sb[g, j][:].indirect(offs_sb[:, slot // PER_COLUMN : (slot + width) // PER_COLUMN]),
                        gate_sb[:, slot : slot + width],
                        MULT,
                    )

        def tokens(pair, g):
            if pair == 0:
                own = ring.tile([P, PAIR * PACK], BF16, name="xb", bufs=1, align_bytes=64)
                xb = own[:]
            else:
                xb = w1_raw[g, 0][:, g * H : (g + 1) * H].bitcast(BF16)
            copy = nc.vector.tensor_copy if (pair, g) == (0, G - 1) else nc.scalar.copy
            width = gather_width(pair, g)
            for s0 in range(0, PAIR, width):
                cols = slice(PACK * s0, PACK * (s0 + width))
                copy(
                    xb[:, cols].rearrange("p (c r j) -> p c j r", r=RUN, j=PACK),
                    picked[pair, g][:, cols].rearrange("p (j c r) -> p c j r", r=RUN, j=PACK),
                )
            quantised = quantize(xb, PAIR, "xq", 2 * G)
            for i in range(2):
                xq[2 * pair + i, g] = columns(quantised, i * C, C)

        def weights1(e, g):
            wb = ring.tile([P, PACK * H], BF16, name="stage", bufs=STAGE_BUFS, align_bytes=64)
            chunk = e * G + g
            if chunk == VECTOR_ALONE:
                nc.vector.tensor_copy(
                    wb[:].rearrange("p (t m j) -> p m j t", t=PACK, j=PACK),
                    w1_raw[e, g][:].rearrange("p (j m t) -> p m j t", j=PACK, t=PACK),
                )
            else:
                src = w1_raw[e, g][:].rearrange("p (j m a b) -> p a m j b", j=PACK, a=2, b=2)
                dst = wb[:].rearrange("p (a b m j) -> p a m j b", a=2, b=2, j=PACK)
                if chunk < SCALAR_ALONE:
                    nc.scalar.copy(dst, src)
                else:
                    nc.vector.tensor_copy(dst[:, 0], src[:, 0])
                    nc.scalar.copy(dst[:, 1], src[:, 1])
            quantised = quantize(wb[:], H, "w1q", W1_CODE_BUFS)
            for u in range(G):
                for t in range(PACK):
                    w1q[e, g, u, t] = columns(quantised, (t * G + u) * P, P)

        def weights1_half(e, g, u):
            wb = ring.tile([P, PACK * KP], BF16, name="stage", bufs=STAGE_BUFS, align_bytes=64)
            src = w1_raw[e, g][:].rearrange("p (j u m t) -> p u m j t", j=PACK, u=G, t=PACK)
            dst = wb[:].rearrange("p (t m j) -> p m j t", t=PACK, j=PACK)
            nc.vector.tensor_copy(dst[:, :, :, 0:2], src[:, u, :, :, 0:2])
            nc.scalar.copy(dst[:, :, :, 2:4], src[:, u, :, :, 2:4])
            quantised = quantize(wb[:], KP, "w1q", W1_CODE_BUFS)
            for t in range(PACK):
                w1q[e, g, u, t] = columns(quantised, t * P, P)

        def first_layer(e, u, hb):
            hb_view = hb.rearrange("p (c t) -> p c t", t=PACK)
            for s0 in range(0, C, P):
                acc = psum.tile([P, PACK, P], F32, name="acc", bufs=ACC_BANKS)
                for t in range(PACK):
                    for g in reversed(range(G)):
                        multiply(acc[:, t, :], w1q[e, g, u, t], columns(xq[e, g], s0, P), g == G - 1, g == 0)
                nc.scalar.activation(hb_view[:, s0 : s0 + P, :], acc[:].rearrange("p t s -> p s t"), GELU)

        def hidden(e, spent):
            hb = spent.bitcast(BF16)
            for u in range(G):
                first_layer(e, u, hb[:, u * C * PACK : (u + 1) * C * PACK])
            quantised = quantize(hb, G * C, "hq", E - 1)
            for u in range(G):
                hq[e, u] = columns(quantised, u * C, C)

        def hidden_half(e, u):
            hb = ring.tile([P, C * PACK], BF16, name="hb_half", bufs=G, align_bytes=64)
            first_layer(e, u, hb[:])
            hq[e, u] = columns(quantize(hb[:], C, "hq_half", G), 0, C)

        def second_layer(e):
            wb = ring.tile([P, G, N, PACK], BF16, name="w2b", bufs=2, align_bytes=64)
            copy = nc.scalar.copy if e == 0 else nc.vector.tensor_copy
            copy(
                wb[:].rearrange("p u (c r) j -> p u c j r", r=RUN),
                w2_view[:, e].rearrange("p u j (c r) -> p u c j r", r=RUN),
            )
            w2q = quantize(wb[:].rearrange("p u n j -> p (u n j)"), G * N, "w2q", E)
            acc = psum.tile([P, C], F32, name="y_acc", bufs=2)
            for u in reversed(range(G)):
                multiply(acc[:], columns(w2q, u * N, N), hq[e, u], u == G - 1, u == 0)
            nc.scalar.copy(y_sb[:, e * C : (e + 1) * C], acc[:])

        for g in range(G):
            for pair in range(E // 2):
                gather(pair, g)
        for pair in range(E // 2):
            for g in range(G):
                tokens(pair, g)
                weights1(pair, g)
        free_part = slice(2 * H, 3 * H)
        weights1(2, 0)
        hidden(0, picked[1, G - 1][:, 0:H])
        weights1(2, 1)
        weights1(3, 0)
        hidden(1, w1_raw[2, 1][:, free_part])
        hidden(2, w1_raw[3, 0][:, free_part])
        for u in range(G):
            weights1_half(E - 1, G - 1, u)
            hidden_half(E - 1, u)
        for e in range(E):
            second_layer(e)

        half = T // 2
        for t0 in range(0, T, half):
            first = ring.tile([P, half], F32, name="first", bufs=2)
            both = ring.tile([P, half], F32, name="both", bufs=2)
            entries = slice(t0 // PER_COLUMN, (t0 + half) // PER_COLUMN)
            nc.vector.tensor_copy(first[:], y_sb[:].indirect(pos1_sb[:, entries]))
            nc.vector.tensor_tensor(both[:], y_sb[:].indirect(pos2_sb[:, entries]), first[:], ADD)
            nc.sync.dma_start(out[:, t0 : t0 + half], both[:])
